import numpy as np
import ml_dtypes


def mxq(x, axis, fmt="e4m3"):
    dtype, down = {"e4m3": (ml_dtypes.float8_e4m3fn, 7), "e5m2": (ml_dtypes.float8_e5m2, 14)}[fmt]
    v = np.moveaxis(np.asarray(x, np.float32).astype(ml_dtypes.bfloat16).astype(np.float64), axis, -1)
    blocks = v.reshape(v.shape[:-1] + (-1, 32))
    amax = np.abs(blocks).max(-1, keepdims=True)
    byte = np.maximum(np.where(amax > 0, np.frexp(amax)[1] - 1 + 127, 0) - down, 1)
    scale = np.exp2(byte - 127.0)
    codes = (blocks / scale).astype(np.float32).astype(dtype).astype(np.float64)
    return np.moveaxis((codes * scale).reshape(v.shape), -1, axis)


WIDE = False


def mx_kscale(k):
    if not WIDE:
        return np.ones(k)
    levels = np.array([10, -10, 5, -5, 0])
    if k % 512:
        return np.exp2(np.random.permutation(np.resize(levels, k // 32))).repeat(32)
    a = np.empty((k // 512, 16))
    for p in range(k // 512):
        a[p, :8] = np.random.permutation(np.resize(levels, 8))
        for g in range(8):
            far = levels[np.abs(levels - a[p, g]) >= 10]
            a[p, g + 8] = far[np.random.randint(len(far))]
    return np.exp2(a.ravel()).repeat(32)


def f64(x):
    return np.asarray(x).astype(np.float64)


def striped(idx):
    return np.tile(idx.reshape(-1, 16).T, (8, 1)).astype(np.uint16)


def unstriped(offs):
    return offs[:16].T.reshape(-1).astype(np.int64)


E2M1 = np.array([0.0, 0.5, 1.0, 1.5, 2.0, 3.0, 4.0, 6.0, -0.0, -0.5, -1.0, -1.5, -2.0, -3.0, -4.0, -6.0])


def pack_weight(w, fmt):
    k, n = w.shape
    w = f64(np.asarray(w, np.float32).astype(ml_dtypes.bfloat16)).reshape(k // 32, 32, n)
    amax = np.abs(w).max(1)
    if fmt == "e4m3":
        byte = np.frexp(amax)[1] - 1 + 127 - 7
    else:
        mant, ex = np.frexp(amax / 6.0)
        byte = np.where(mant > 0.5, ex, ex - 1) + 127
    byte = np.clip(np.where(amax > 0, byte, 1), 1, 254)
    scaled = (w * np.exp2(127.0 - byte)[:, None, :]).reshape(k, n).astype(np.float32)
    by_word = np.ascontiguousarray(scaled.reshape(k // 512, 128, 4, n).transpose(0, 1, 3, 2))
    if fmt == "e4m3":
        words = by_word.astype(ml_dtypes.float8_e4m3fn).view(np.uint8)
    else:
        c = by_word.astype(ml_dtypes.float4_e2m1fn).view(np.uint8) & 0xF
        words = (c[..., 0::2] | (c[..., 1::2] << 4)).reshape(k // 512, 128, 2 * n)
    return np.ascontiguousarray(words), np.ascontiguousarray(byte.astype(np.uint8).reshape(k // 512, 16, n))


def unpack_weight(words, scales, fmt):
    g, _, n = scales.shape
    words = np.ascontiguousarray(words).reshape(g, 128, n, -1)
    if fmt == "e4m3":
        vals = words.view(ml_dtypes.float8_e4m3fn).astype(np.float64)
    else:
        nib = np.empty((g, 128, n, 4), np.uint8)
        nib[..., 0::2] = words & 0xF
        nib[..., 1::2] = words >> 4
        vals = E2M1[nib]
    vals = vals * np.repeat(np.exp2(scales.astype(np.float64) - 127.0), 8, axis=1)[..., None]
    return vals.transpose(0, 1, 3, 2).reshape(g * 512, n)


def relu2(v):
    return np.maximum(v, 0.0) ** 2


K, T, E, C, H, N = 1024, 512, 8, 128, 512, 384
TOP = 4
PAD = 64


def by_expert(wq, xq):
    return np.concatenate([wq[e].T @ xq[:, e * C:(e + 1) * C] for e in range(E)], axis=1)


def setup_inputs():
    n = np.random.standard_normal
    s = mx_kscale(K)[:, None]
    u = mx_kscale(H)
    slot_token = np.empty(E * C, np.int64); pos = np.tile(E * C + np.arange(T) % PAD, (TOP, 1)); taken = np.zeros(T, np.int64)
    liked = np.random.randn(T)
    for e in np.random.permutation(E):
        free = np.flatnonzero(taken < TOP); pick = np.random.permutation(free[np.argsort(-(liked[free] + np.random.gumbel(size=free.size)))[:C]]); slot_token[e * C:(e + 1) * C] = pick
        pos[taken[pick], pick] = e * C + np.arange(C); taken[pick] += 1
    g = np.random.uniform(0.2, 0.8, (TOP, T))
    w1 = [pack_weight(m, "e2m1") for m in n((E, K, H)) / np.sqrt(K) / s[None] * u[None, None, :]]
    w2 = [pack_weight(m, "e2m1") for m in n((E, H, N)) / np.sqrt(H) / u[None, :, None] ** 2]
    x = pack_weight(n((K, T)) * s, "e4m3")
    return {
        "x_words": x[0],
        "x_scales": x[1],
        "w1_words": np.stack([m[0] for m in w1]),
        "w1_scales": np.stack([m[1] for m in w1]),
        "w2_words": np.stack([m[0] for m in w2]),
        "w2_scales": np.stack([m[1] for m in w2]),
        "gate": np.stack([np.tile(r, (N, 1)) for r in g]).astype(np.float32),
        "offs": striped(slot_token),
        "pos1": striped(pos[0]),
        "pos2": striped(pos[1]),
        "pos3": striped(pos[2]),
        "pos4": striped(pos[3]),
    }


def reference(x_words, x_scales, w1_words, w1_scales, w2_words, w2_scales, gate, offs, pos1, pos2, pos3, pos4):
    idx = unstriped(offs)
    w1 = np.stack([unpack_weight(w1_words[e], w1_scales[e], "e2m1") for e in range(E)])
    w2 = np.stack([unpack_weight(w2_words[e], w2_scales[e], "e2m1") for e in range(E)])
    xq = unpack_weight(x_words, x_scales, "e4m3")[:, idx]
    h = relu2(by_expert(w1, xq))
    y = by_expert(w2, mxq(h, 0, "e4m3"))
    y = np.concatenate([y, np.zeros((N, PAD))], axis=1)
    return sum(f64(gate[r]) * y[:, unstriped(p)] for r, p in enumerate((pos1, pos2, pos3, pos4)))

@@ -1,0 +1,256 @@
+from contextlib import ExitStack
+
+import concourse.mybir as mybir
+from concourse.masks import make_identity
+
+K, T, E, C, H, N = 1024, 512, 8, 128, 512, 384
+TOP = 4
+PAD = 64
+P = 128
+PASSES = K // 512
+BLOCKS = N // P
+SLOTS = E * C
+HALF = 256
+CHUNKS = T // P
+FLOPS = 2 * SLOTS * (K * H + H * N)
+
+F32 = mybir.dt.float32
+BF16 = mybir.dt.bfloat16
+I32 = mybir.dt.int32
+U32 = mybir.dt.uint32
+U16 = mybir.dt.uint16
+U8 = mybir.dt.uint8
+FP8X4 = mybir.dt.float8_e4m3fn_x4
+FP4X4 = mybir.dt.float4_e2m1fn_x4
+ACT = mybir.ActivationFunctionType
+ALU = mybir.AluOpType
+
+GATHER_GROUPS = [(0, 1), (1, 2), (2, 4), (4, 6), (6, 8)]
+RELU_ON_VECTOR = (7,)
+COPY_ON_VECTOR = (4, 5, 7)
+LAG = 3
+WORD_GROUPS = [(0, 1), (1, 3), (3, 5), (5, 8)]
+SCALE_GROUPS = [(0, 2), (2, 8)]
+
+
+def tile_moe_ecr_mlp_relu2_kernel(
+    tc, x_words, x_scales, w1_words, w1_scales, w2_words, w2_scales, gate, offs, pos1, pos2, pos3, pos4, out
+):
+    nc = tc.nc
+    with ExitStack() as ctx:
+        keep = ctx.enter_context(tc.tile_pool(name="keep", bufs=1))
+        ring = ctx.enter_context(tc.tile_pool(name="ring", bufs=4))
+        pair = ctx.enter_context(tc.tile_pool(name="pair", bufs=2))
+        psum = ctx.enter_context(tc.psum_pool(name="psum", bufs=1))
+
+        offs_t = keep.tile([P, SLOTS // 16], U16, name="offs_t")
+        pos_t = [keep.tile([P, T // 16], U16, name="pos_t%d" % r) for r in range(TOP)]
+        xw = keep.tile([P, PASSES * T], I32, name="xw", align_bytes=64)
+        xs = keep.tile([P, PASSES * T], U8, name="xs", align_bytes=64)
+        w1s = [
+            keep.tile([P, (hi - lo) * PASSES * H], U8, name="w1s%d" % lo, align_bytes=64) for lo, hi in SCALE_GROUPS
+        ]
+        w1w = [
+            keep.tile([P, (hi - lo) * PASSES * 2 * H], U8, name="w1w%d" % lo, align_bytes=64) for lo, hi in WORD_GROUPS
+        ]
+        w2s = keep.tile([P, E * N], U8, name="w2s", align_bytes=64)
+        w2w = keep.tile([P, E * 2 * N], U8, name="w2w", align_bytes=64)
+        y = keep.tile([P, BLOCKS, SLOTS + PAD], F32, name="y", align_bytes=64)
+        gate_rows = keep.tile([P, P], F32, name="gate_rows")
+        gate_cols = keep.tile([P, TOP * 4], F32, name="gate_cols")
+        ident = keep.tile([P, P], F32, name="ident")
+        clock = keep.tile([P, 8], F32, name="clock")
+
+        nc.gpsimd.memset(xs[:].bitcast(I32), 0)
+        nc.vector.memset(w1s[0][:].bitcast(I32), 0)
+        nc.vector.memset(w1s[1][:].bitcast(I32), 0)
+        nc.gpsimd.memset(w2s[:].bitcast(I32), 0)
+        make_identity(nc, ident[:])
+        nc.gpsimd.memset(gate_rows[:], 0.0)
+        nc.gpsimd.memset(y[:, :, SLOTS:], 0.0)
+
+        def load_scales(plane, rows):
+            for r in range(4):
+                src = rows[r].bitcast(I32)
+                dst = plane[r:P:32, :].bitcast(I32).rearrange("q (g w) -> q g w", g=src.shape[1])
+                nc.sync.dma_start(out=dst, in_=src)
+
+        def load_words(tile, src):
+            nc.sync.dma_start(
+                out=tile[:].bitcast(I32).rearrange("p (g w) -> p g w", g=src.shape[0] * src.shape[1]),
+                in_=src.rearrange("e s p w -> p (e s) w").bitcast(I32),
+            )
+
+        def load_w1_words(g):
+            lo, hi = WORD_GROUPS[g]
+            load_words(w1w[g], w1_words[lo:hi])
+
+        def load_w1_scales(g):
+            lo, hi = SCALE_GROUPS[g]
+            load_scales(w1s[g], w1_scales[lo:hi].rearrange("e s (q r) i -> r q (e s) i", r=4))
+
+        nc.sync.dma_start(out=offs_t[:], in_=offs)
+        nc.sync.dma_start(
+            out=xw[:].rearrange("p (s t) -> p s t", s=PASSES),
+            in_=x_words.rearrange("s p t r -> p s (t r)").bitcast(I32),
+        )
+        load_w1_words(0)
+        load_scales(xs, x_scales.rearrange("s (q r) t -> r q s t", r=4))
+        load_w1_scales(0)
+        load_w1_words(1)
+        load_w1_scales(1)
+        load_w1_words(2)
+        load_w1_words(3)
+        load_scales(w2s, w2_scales.rearrange("e o (q r) n -> r q (e o) n", r=4))
+        load_words(w2w, w2_words)
+        for tile_r, src in zip(pos_t, (pos1, pos2, pos3, pos4)):
+            nc.sync.dma_start(out=tile_r[:], in_=src)
+        step_rows = N + 1
+        nc.gpsimd.dma_start(
+            out=gate_rows[: TOP * 4, :],
+            in_=gate.rearrange("r n (c p) -> (r n c) p", p=P)[::step_rows, :],
+        )
+
+        w1_word = {}
+        w1_scale = {}
+        for g, (lo, hi) in enumerate(WORD_GROUPS):
+            for e in range(lo, hi):
+                for s in range(PASSES):
+                    col = ((e - lo) * PASSES + s) * 2 * H
+                    w1_word[e, s] = w1w[g][:, col : col + 2 * H]
+        for g, (lo, hi) in enumerate(SCALE_GROUPS):
+            for e in range(lo, hi):
+                for s in range(PASSES):
+                    col = ((e - lo) * PASSES + s) * H
+                    w1_scale[e, s] = w1s[g][:, col : col + H]
+
+        words = {}
+        scales = {}
+        def gather(lo, hi):
+            idx = offs_t[:, lo * C // 16 : hi * C // 16]
+            gw = pair.tile([P, PASSES, (hi - lo) * C], U32, name="gw", align_bytes=64)
+            gs = pair.tile([P, PASSES, (hi - lo) * C], U8, name="gs", align_bytes=64)
+            for s in range(PASSES):
+                nc.vector.tensor_copy(gw[:, s, :], xw[:, s * T : (s + 1) * T].bitcast(U32).indirect(idx))
+            for s in range(PASSES):
+                nc.vector.tensor_copy(gs[:, s, :], xs[:, s * T : (s + 1) * T].indirect(idx))
+            for e in range(lo, hi):
+                for s in range(PASSES):
+                    words[e, s] = gw[:, s, (e - lo) * C : (e - lo + 1) * C]
+                    scales[e, s] = gs[:, s, (e - lo) * C : (e - lo + 1) * C]
+
+        relu = {}
+        hq = {}
+
+        def first_layer(e):
+            acc = psum.tile([P, H], F32, name="acc", tag="a", bufs=3)
+            for s in range(PASSES):
+                nc.tensor.matmul_mx(
+                    out=acc[:],
+                    lhsT=words[e, s].bitcast(FP8X4),
+                    lhsT_scale=scales[e, s],
+                    rhs=w1_word[e, s].bitcast(FP4X4),
+                    rhs_scale=w1_scale[e, s],
+                    start=(s == 0),
+                    stop=(s == PASSES - 1),
+                )
+            relu[e] = ring.tile([P, 4, P], F32, name="relu")
+            if e in RELU_ON_VECTOR:
+                nc.vector.tensor_scalar_max(relu[e][:], acc[:].rearrange("c (m d) -> c d m", d=4), 0.0)
+            else:
+                nc.scalar.activation(relu[e][:], acc[:].rearrange("c (m d) -> c d m", d=4), ACT.Relu)
+
+        def turn(e):
+            turned = psum.tile([P, 4, C], F32, name="turned", tag="b", bufs=3)
+            for d in range(4):
+                nc.tensor.transpose(turned[:, d, :], relu[e][:, d, :], ident[:])
+            h = keep.tile([P, C, 4], BF16, name="h%d" % e, align_bytes=64)
+            nc.scalar.activation(h[:], turned[:].rearrange("p d c -> p c d"), ACT.Square)
+            codes = keep.tile([P, C], U32, name="codes%d" % e, align_bytes=64)
+            plane = keep.tile([P, C], U8, name="plane%d" % e, align_bytes=64)
+            nc.vector.quantize_mx(out=codes[:].bitcast(FP8X4), scales=plane[:], in_=h[:].rearrange("p c d -> p (c d)"))
+            hq[e] = (codes, plane)
+
+        def second_layer(e):
+            acc2 = psum.tile([P, BLOCKS, C], F32, name="acc2", tag="c", bufs=2)
+            codes, plane = hq[e]
+            for b in range(BLOCKS):
+                col = e * N + b * P
+                nc.tensor.matmul_mx(
+                    out=acc2[:, b, :],
+                    lhsT=w2w[:, 2 * col : 2 * (col + P)].bitcast(FP4X4),
+                    lhsT_scale=w2s[:, col : col + P],
+                    rhs=codes[:].bitcast(FP8X4),
+                    rhs_scale=plane[:],
+                    start=True,
+                    stop=True,
+                )
+            if e in COPY_ON_VECTOR:
+                nc.vector.tensor_copy(y[:, :, e * C : (e + 1) * C], acc2[:])
+            else:
+                nc.scalar.copy(y[:, :, e * C : (e + 1) * C], acc2[:])
+
+        starts = dict(GATHER_GROUPS)
+        for step in range(E + LAG):
+            if step in starts:
+                gather(step, starts[step])
+            if step < E:
+                first_layer(step)
+            if 1 <= step <= E:
+                turn(step - 1)
+            if step >= LAG:
+                second_layer(step - LAG)
+        nc.gpsimd.tensor_copy(clock[:, 0:1], y[:, 2, SLOTS - 1 : SLOTS])
+
+        gate_ps = psum.tile([P, P], F32, name="gate_ps", tag="c", bufs=2)
+        nc.tensor.transpose(gate_ps[:], gate_rows[:], ident[:])
+        nc.scalar.copy(gate_cols[:], gate_ps[:, : TOP * 4])
+
+        out_v = out.rearrange("(b n) t -> n b t", n=P)
+        picked = [keep.tile([P, BLOCKS, T], F32, name="picked%d" % r) for r in range(TOP)]
+        cuts = [(r, 0, T) for r in range(TOP - 1)] + [(TOP - 1, 0, HALF), (TOP - 1, HALF, T)]
+        for r, lo, hi in cuts:
+            for b in range(BLOCKS):
+                nc.vector.tensor_copy(picked[r][:, b, lo:hi], y[:, b, :].indirect(pos_t[r][:, lo // 16 : hi // 16]))
+
+        units = [(r, c) for r in range(TOP) for c in range(CHUNKS)]
+        gated = {}
+        sums = [psum.tile([P, BLOCKS, P], F32, name="sums%d" % c, tag="b", bufs=3) for c in range(3)]
+        sums.append(psum.tile([P, BLOCKS, P], F32, name="sums3", tag="c", bufs=2))
+
+        def weigh(unit):
+            r, c = unit
+            by_token = psum.tile([P, BLOCKS, P], F32, name="by_token", tag="a", bufs=3)
+            for b in range(BLOCKS):
+                nc.tensor.transpose(by_token[:, b, :], picked[r][:, b, c * P : (c + 1) * P], ident[:])
+            gated[unit] = ring.tile([P, BLOCKS, P], F32, name="gated")
+            col = r * CHUNKS + c
+            if unit == units[-1]:
+                nc.vector.tensor_scalar(gated[unit][:], by_token[:], gate_cols[:, col : col + 1], None, ALU.mult)
+            else:
+                nc.scalar.activation(gated[unit][:], by_token[:], ACT.Copy, scale=gate_cols[:, col : col + 1])
+
+        def add_up(unit):
+            r, c = unit
+            for b in range(BLOCKS):
+                nc.tensor.matmul(
+                    sums[c][:, b, :],
+                    lhsT=gated[unit][:, b, :],
+                    rhs=ident[:],
+                    is_transpose=True,
+                    start=(r == 0 and b == 0),
+                    stop=(r == TOP - 1 and b == BLOCKS - 1),
+                )
+            if r == TOP - 1:
+                res = ring.tile([P, BLOCKS, P], F32, name="res")
+                if unit == units[-1]:
+                    nc.vector.tensor_copy(res[:], sums[c][:])
+                else:
+                    nc.scalar.copy(res[:], sums[c][:])
+                nc.sync.dma_start(out=out_v[:, :, c * P : (c + 1) * P], in_=res[:])
+
+        for i in range(len(units) + 2):
+            if i < len(units):
+                weigh(units[i])
+            if i >= 2:
+                add_up(units[i - 2])

@@ -25,12 +25,12 @@ FP4X4 = mybir.dt.float4_e2m1fn_x4
 ACT = mybir.ActivationFunctionType
 ALU = mybir.AluOpType
 
-GATHER_GROUPS = [(0, 1), (1, 2), (2, 4), (4, 6), (6, 8)]
+WORD_GATHERS = [(0, 1), (1, 2), (2, 4), (4, 6), (6, 8)]
+BYTE_GATHERS = [(0, 2), (2, 4), (4, 6), (6, 8)]
+QUANT_GROUPS = [(0, 4), (4, 6), (6, 7), (7, 8)]
 RELU_ON_VECTOR = (7,)
-COPY_ON_VECTOR = (4, 5, 7)
-LAG = 3
 WORD_GROUPS = [(0, 1), (1, 3), (3, 5), (5, 8)]
-SCALE_GROUPS = [(0, 2), (2, 8)]
+EARLY = 2
 
 
 def tile_moe_ecr_mlp_relu2_kernel(
@@ -40,34 +40,29 @@ def tile_moe_ecr_mlp_relu2_kernel(
     with ExitStack() as ctx:
         keep = ctx.enter_context(tc.tile_pool(name="keep", bufs=1))
         ring = ctx.enter_context(tc.tile_pool(name="ring", bufs=4))
-        pair = ctx.enter_context(tc.tile_pool(name="pair", bufs=2))
+        stream = ctx.enter_context(tc.tile_pool(name="stream", bufs=4))
         psum = ctx.enter_context(tc.psum_pool(name="psum", bufs=1))
 
         offs_t = keep.tile([P, SLOTS // 16], U16, name="offs_t")
         pos_t = [keep.tile([P, T // 16], U16, name="pos_t%d" % r) for r in range(TOP)]
         xw = keep.tile([P, PASSES * T], I32, name="xw", align_bytes=64)
         xs = keep.tile([P, PASSES * T], U8, name="xs", align_bytes=64)
-        w1s = [
-            keep.tile([P, (hi - lo) * PASSES * H], U8, name="w1s%d" % lo, align_bytes=64) for lo, hi in SCALE_GROUPS
-        ]
-        w1w = [
-            keep.tile([P, (hi - lo) * PASSES * 2 * H], U8, name="w1w%d" % lo, align_bytes=64) for lo, hi in WORD_GROUPS
-        ]
+        early = keep.tile([P, EARLY * PASSES * H], U8, name="early", align_bytes=64)
+        late = keep.tile([P, (E - EARLY) * PASSES * H], U8, name="late", align_bytes=64)
         w2s = keep.tile([P, E * N], U8, name="w2s", align_bytes=64)
-        w2w = keep.tile([P, E * 2 * N], U8, name="w2w", align_bytes=64)
         y = keep.tile([P, BLOCKS, SLOTS + PAD], F32, name="y", align_bytes=64)
         gate_rows = keep.tile([P, P], F32, name="gate_rows")
-        gate_cols = keep.tile([P, TOP * 4], F32, name="gate_cols")
+        gate_cols = keep.tile([P, TOP * CHUNKS], F32, name="gate_cols")
         ident = keep.tile([P, P], F32, name="ident")
-        clock = keep.tile([P, 8], F32, name="clock")
 
         nc.gpsimd.memset(xs[:].bitcast(I32), 0)
-        nc.vector.memset(w1s[0][:].bitcast(I32), 0)
-        nc.vector.memset(w1s[1][:].bitcast(I32), 0)
-        nc.gpsimd.memset(w2s[:].bitcast(I32), 0)
+        nc.vector.memset(early[:].bitcast(I32), 0)
+        nc.vector.memset(late[:, :2560].bitcast(I32), 0)
+        nc.gpsimd.memset(late[:, 2560:].bitcast(I32), 0)
+        nc.vector.memset(w2s[:].bitcast(I32), 0)
         make_identity(nc, ident[:])
-        nc.gpsimd.memset(gate_rows[:], 0.0)
-        nc.gpsimd.memset(y[:, :, SLOTS:], 0.0)
+        nc.vector.memset(gate_rows[:], 0.0)
+        nc.vector.memset(y[:, :, SLOTS:], 0.0)
 
         def load_scales(plane, rows):
             for r in range(4):
@@ -75,75 +70,70 @@ def tile_moe_ecr_mlp_relu2_kernel(
                 dst = plane[r:P:32, :].bitcast(I32).rearrange("q (g w) -> q g w", g=src.shape[1])
                 nc.sync.dma_start(out=dst, in_=src)
 
-        def load_words(tile, src):
+        def load_words(src):
+            groups = src.shape[0] * src.shape[1]
+            tile = stream.tile([P, groups * src.shape[3]], U8, name="weights", align_bytes=64)
             nc.sync.dma_start(
-                out=tile[:].bitcast(I32).rearrange("p (g w) -> p g w", g=src.shape[0] * src.shape[1]),
+                out=tile[:].bitcast(I32).rearrange("p (g w) -> p g w", g=groups),
                 in_=src.rearrange("e s p w -> p (e s) w").bitcast(I32),
             )
+            return tile
 
-        def load_w1_words(g):
-            lo, hi = WORD_GROUPS[g]
-            load_words(w1w[g], w1_words[lo:hi])
+        w1_word = {}
+        w1_scale = {}
 
-        def load_w1_scales(g):
-            lo, hi = SCALE_GROUPS[g]
-            load_scales(w1s[g], w1_scales[lo:hi].rearrange("e s (q r) i -> r q (e s) i", r=4))
+        def load_w1_words(lo, hi):
+            tile = load_words(w1_words[lo:hi])
+            for e in range(lo, hi):
+                for s in range(PASSES):
+                    col = ((e - lo) * PASSES + s) * 2 * H
+                    w1_word[e, s] = tile[:, col : col + 2 * H]
 
-        nc.sync.dma_start(out=offs_t[:], in_=offs)
+        def load_w1_scales(plane, lo, hi):
+            load_scales(plane, w1_scales[lo:hi].rearrange("e s (q r) i -> r q (e s) i", r=4))
+            for e in range(lo, hi):
+                for s in range(PASSES):
+                    col = ((e - lo) * PASSES + s) * H
+                    w1_scale[e, s] = plane[:, col : col + H]
+
         nc.sync.dma_start(
             out=xw[:].rearrange("p (s t) -> p s t", s=PASSES),
             in_=x_words.rearrange("s p t r -> p s (t r)").bitcast(I32),
         )
-        load_w1_words(0)
+        nc.sync.dma_start(out=offs_t[:], in_=offs)
+        nc.sync.dma_start(out=pos_t[0][:], in_=pos1)
         load_scales(xs, x_scales.rearrange("s (q r) t -> r q s t", r=4))
-        load_w1_scales(0)
-        load_w1_words(1)
-        load_w1_scales(1)
-        load_w1_words(2)
-        load_w1_words(3)
+        load_w1_words(0, 1)
+        load_w1_scales(early, 0, EARLY)
+        load_w1_words(1, 3)
+        load_w1_scales(late, EARLY, E)
+        load_w1_words(3, 5)
+        load_w1_words(5, E)
         load_scales(w2s, w2_scales.rearrange("e o (q r) n -> r q (e o) n", r=4))
-        load_words(w2w, w2_words)
-        for tile_r, src in zip(pos_t, (pos1, pos2, pos3, pos4)):
+        for tile_r, src in zip(pos_t[1:], (pos2, pos3, pos4)):
             nc.sync.dma_start(out=tile_r[:], in_=src)
-        step_rows = N + 1
-        nc.gpsimd.dma_start(
-            out=gate_rows[: TOP * 4, :],
-            in_=gate.rearrange("r n (c p) -> (r n c) p", p=P)[::step_rows, :],
+        nc.sync.dma_start(
+            out=gate_rows[: TOP * CHUNKS, :],
+            in_=gate.rearrange("r n (c p) -> (r n c) p", p=P)[:: N + 1, :],
         )
-
-        w1_word = {}
-        w1_scale = {}
-        for g, (lo, hi) in enumerate(WORD_GROUPS):
-            for e in range(lo, hi):
-                for s in range(PASSES):
-                    col = ((e - lo) * PASSES + s) * 2 * H
-                    w1_word[e, s] = w1w[g][:, col : col + 2 * H]
-        for g, (lo, hi) in enumerate(SCALE_GROUPS):
-            for e in range(lo, hi):
-                for s in range(PASSES):
-                    col = ((e - lo) * PASSES + s) * H
-                    w1_scale[e, s] = w1s[g][:, col : col + H]
 
         words = {}
         scales = {}
-        def gather(lo, hi):
+
+        def gather(found, table, dtype, name, depth, lo, hi):
             idx = offs_t[:, lo * C // 16 : hi * C // 16]
-            gw = pair.tile([P, PASSES, (hi - lo) * C], U32, name="gw", align_bytes=64)
-            gs = pair.tile([P, PASSES, (hi - lo) * C], U8, name="gs", align_bytes=64)
+            tile = ring.tile([P, PASSES, (hi - lo) * C], dtype, name=name, align_bytes=64, bufs=depth)
             for s in range(PASSES):
-                nc.vector.tensor_copy(gw[:, s, :], xw[:, s * T : (s + 1) * T].bitcast(U32).indirect(idx))
-            for s in range(PASSES):
-                nc.vector.tensor_copy(gs[:, s, :], xs[:, s * T : (s + 1) * T].indirect(idx))
-            for e in range(lo, hi):
-                for s in range(PASSES):
-                    words[e, s] = gw[:, s, (e - lo) * C : (e - lo + 1) * C]
-                    scales[e, s] = gs[:, s, (e - lo) * C : (e - lo + 1) * C]
+                nc.vector.tensor_copy(tile[:, s, :], table[:, s * T : (s + 1) * T].indirect(idx))
+                for e in range(lo, hi):
+                    found[e, s] = tile[:, s, (e - lo) * C : (e - lo + 1) * C]
 
         relu = {}
         hq = {}
+        hidden = {}
 
         def first_layer(e):
-            acc = psum.tile([P, H], F32, name="acc", tag="a", bufs=3)
+            acc = psum.tile([P, H], F32, name="acc", tag="a", bufs=2)
             for s in range(PASSES):
                 nc.tensor.matmul_mx(
                     out=acc[:],
@@ -161,96 +151,136 @@ def tile_moe_ecr_mlp_relu2_kernel(
                 nc.scalar.activation(relu[e][:], acc[:].rearrange("c (m d) -> c d m", d=4), ACT.Relu)
 
         def turn(e):
-            turned = psum.tile([P, 4, C], F32, name="turned", tag="b", bufs=3)
+            turned = psum.tile([P, 4, C], F32, name="turned", tag="b", bufs=2)
             for d in range(4):
                 nc.tensor.transpose(turned[:, d, :], relu[e][:, d, :], ident[:])
-            h = keep.tile([P, C, 4], BF16, name="h%d" % e, align_bytes=64)
-            nc.scalar.activation(h[:], turned[:].rearrange("p d c -> p c d"), ACT.Square)
-            codes = keep.tile([P, C], U32, name="codes%d" % e, align_bytes=64)
-            plane = keep.tile([P, C], U8, name="plane%d" % e, align_bytes=64)
-            nc.vector.quantize_mx(out=codes[:].bitcast(FP8X4), scales=plane[:], in_=h[:].rearrange("p c d -> p (c d)"))
-            hq[e] = (codes, plane)
-
-        def second_layer(e):
-            acc2 = psum.tile([P, BLOCKS, C], F32, name="acc2", tag="c", bufs=2)
-            codes, plane = hq[e]
-            for b in range(BLOCKS):
-                col = e * N + b * P
-                nc.tensor.matmul_mx(
-                    out=acc2[:, b, :],
-                    lhsT=w2w[:, 2 * col : 2 * (col + P)].bitcast(FP4X4),
-                    lhsT_scale=w2s[:, col : col + P],
-                    rhs=codes[:].bitcast(FP8X4),
-                    rhs_scale=plane[:],
-                    start=True,
-                    stop=True,
+            lo, hi = [g for g in QUANT_GROUPS if g[0] <= e < g[1]][0]
+            if e == lo:
+                hidden[lo] = keep.tile([P, hi - lo, C, 4], BF16, name="h%d" % e, align_bytes=64)
+            nc.scalar.activation(hidden[lo][:, e - lo, :, :], turned[:].rearrange("p d c -> p c d"), ACT.Square)
+            if e == hi - 1:
+                codes = keep.tile([P, (hi - lo) * C], U32, name="codes%d" % e, align_bytes=64)
+                plane = keep.tile([P, (hi - lo) * C], U8, name="plane%d" % e, align_bytes=64)
+                nc.vector.quantize_mx(
+                    out=codes[:].bitcast(FP8X4), scales=plane[:], in_=hidden[lo][:].rearrange("p e c d -> p (e c d)")
                 )
-            if e in COPY_ON_VECTOR:
-                nc.vector.tensor_copy(y[:, :, e * C : (e + 1) * C], acc2[:])
-            else:
-                nc.scalar.copy(y[:, :, e * C : (e + 1) * C], acc2[:])
+                for k in range(lo, hi):
+                    cols = slice((k - lo) * C, (k - lo + 1) * C)
+                    hq[k] = (codes[:, cols], plane[:, cols])
 
-        starts = dict(GATHER_GROUPS)
-        for step in range(E + LAG):
-            if step in starts:
-                gather(step, starts[step])
+        def second_layer(tag, depth, blocks, pieces):
+            lo, hi = pieces[0][1], pieces[-1][2]
+            bank = psum.tile([P, len(blocks), (hi - lo) * C], F32, name="acc2", tag=tag, bufs=depth)
+            for copy, first, end in pieces:
+                for e in range(first, end):
+                    codes, plane = hq[e]
+                    for b in blocks:
+                        col = e * N + b * P
+                        nc.tensor.matmul_mx(
+                            out=bank[:, b - blocks[0], (e - lo) * C : (e - lo + 1) * C],
+                            lhsT=w2w[:, 2 * col : 2 * (col + P)].bitcast(FP4X4),
+                            lhsT_scale=w2s[:, col : col + P],
+                            rhs=codes.bitcast(FP8X4),
+                            rhs_scale=plane,
+                            start=True,
+                            stop=True,
+                        )
+                copy(y[:, blocks[0] : blocks[-1] + 1, first * C : end * C], bank[:, :, (first - lo) * C : (end - lo) * C])
+
+        word_starts = dict(WORD_GATHERS)
+        byte_starts = dict(BYTE_GATHERS)
+        for step in range(E + 1):
+            if step in byte_starts:
+                gather(scales, xs[:], U8, "gs", 2, step, byte_starts[step])
+            if step in word_starts:
+                gather(words, xw[:].bitcast(U32), U32, "gw", 2, step, word_starts[step])
             if step < E:
                 first_layer(step)
+            if step == 0:
+                w2w = load_words(w2_words)
+            if step == 2:
+                gate_last = stream.tile([P, HALF], F32, name="gate_last", tag="weights", align_bytes=64)
+                nc.sync.dma_start(out=gate_last[:], in_=gate[TOP - 1, :P, HALF:])
             if 1 <= step <= E:
                 turn(step - 1)
-            if step >= LAG:
-                second_layer(step - LAG)
-        nc.gpsimd.tensor_copy(clock[:, 0:1], y[:, 2, SLOTS - 1 : SLOTS])
-
-        gate_ps = psum.tile([P, P], F32, name="gate_ps", tag="c", bufs=2)
+        second_layer("c", 4, (0,), [(nc.scalar.copy, 0, 4)])
+        second_layer("a", 2, (0,), [(nc.vector.tensor_copy, 4, 7)])
+        second_layer("c", 4, (0,), [(nc.vector.tensor_copy, 7, 8)])
+        second_layer("b", 2, (1,), [(nc.scalar.copy, 0, 4)])
+        second_layer("b", 2, (2,), [(nc.scalar.copy, 0, 4)])
+        second_layer("c", 4, (1, 2), [(nc.scalar.copy, 4, 6)])
+        second_layer("c", 4, (1, 2), [(nc.scalar.copy, 6, 8)])
+        gate_ps = psum.tile([P, P], F32, name="gate_ps", tag="a", bufs=2)
         nc.tensor.transpose(gate_ps[:], gate_rows[:], ident[:])
-        nc.scalar.copy(gate_cols[:], gate_ps[:, : TOP * 4])
+        nc.scalar.copy(gate_cols[:], gate_ps[:, : TOP * CHUNKS])
 
         out_v = out.rearrange("(b n) t -> n b t", n=P)
-        picked = [keep.tile([P, BLOCKS, T], F32, name="picked%d" % r) for r in range(TOP)]
+        picked = [ring.tile([P, BLOCKS, T], F32, name="picked", bufs=2) for r in range(TOP)]
         cuts = [(r, 0, T) for r in range(TOP - 1)] + [(TOP - 1, 0, HALF), (TOP - 1, HALF, T)]
         for r, lo, hi in cuts:
             for b in range(BLOCKS):
                 nc.vector.tensor_copy(picked[r][:, b, lo:hi], y[:, b, :].indirect(pos_t[r][:, lo // 16 : hi // 16]))
 
-        units = [(r, c) for r in range(TOP) for c in range(CHUNKS)]
+        units = [(r, c) for r in range(TOP) for c in range(CHUNKS)][:-2]
         gated = {}
-        sums = [psum.tile([P, BLOCKS, P], F32, name="sums%d" % c, tag="b", bufs=3) for c in range(3)]
-        sums.append(psum.tile([P, BLOCKS, P], F32, name="sums3", tag="c", bufs=2))
+        sums = [
+            psum.tile([P, 2, HALF], F32, name="sums0", tag="b", bufs=2),
+            psum.tile([P, 1, HALF], F32, name="sums1", tag="b", bufs=2),
+            psum.tile([P, 2, HALF], F32, name="sums2", tag="c", bufs=4),
+            psum.tile([P, 1, HALF], F32, name="sums3", tag="c", bufs=4),
+        ]
+        spans = (slice(0, 2), slice(2, 3))
+
+        first = [psum.tile([P, BLOCKS, P], F32, name="first%d" % c, tag="a", bufs=2) for c in range(2)]
+        first.extend([psum.tile([P, BLOCKS, P], F32, name="first%d" % c, tag="c", bufs=4) for c in (2, 3)])
+        for b in range(BLOCKS):
+            for c in range(CHUNKS):
+                nc.tensor.transpose(first[c][:, b, :], picked[0][:, b, c * P : (c + 1) * P], ident[:])
 
         def weigh(unit):
             r, c = unit
-            by_token = psum.tile([P, BLOCKS, P], F32, name="by_token", tag="a", bufs=3)
-            for b in range(BLOCKS):
-                nc.tensor.transpose(by_token[:, b, :], picked[r][:, b, c * P : (c + 1) * P], ident[:])
+            if r == 0:
+                by_token = first[c]
+            else:
+                if c < 2:
+                    by_token = psum.tile([P, BLOCKS, P], F32, name="by_token", tag="a", bufs=2)
+                else:
+                    by_token = psum.tile([P, BLOCKS, P], F32, name="by_token", tag="c", bufs=4)
+                for b in range(BLOCKS):
+                    nc.tensor.transpose(by_token[:, b, :], picked[r][:, b, c * P : (c + 1) * P], ident[:])
             gated[unit] = ring.tile([P, BLOCKS, P], F32, name="gated")
             col = r * CHUNKS + c
-            if unit == units[-1]:
-                nc.vector.tensor_scalar(gated[unit][:], by_token[:], gate_cols[:, col : col + 1], None, ALU.mult)
-            else:
-                nc.scalar.activation(gated[unit][:], by_token[:], ACT.Copy, scale=gate_cols[:, col : col + 1])
+            nc.scalar.activation(gated[unit][:], by_token[:], ACT.Copy, scale=gate_cols[:, col : col + 1])
 
         def add_up(unit):
             r, c = unit
+            last = TOP - 1 if c < 2 else TOP - 2
             for b in range(BLOCKS):
                 nc.tensor.matmul(
-                    sums[c][:, b, :],
+                    sums[c // 2 * 2 + b // 2][:, b % 2, c % 2 * P : (c % 2 + 1) * P],
                     lhsT=gated[unit][:, b, :],
                     rhs=ident[:],
                     is_transpose=True,
-                    start=(r == 0 and b == 0),
-                    stop=(r == TOP - 1 and b == BLOCKS - 1),
+                    start=(r == 0 and c % 2 == 0 and b != 1),
+                    stop=(r == last and c % 2 == 1 and b != 0),
                 )
-            if r == TOP - 1:
-                res = ring.tile([P, BLOCKS, P], F32, name="res")
-                if unit == units[-1]:
-                    nc.vector.tensor_copy(res[:], sums[c][:])
-                else:
-                    nc.scalar.copy(res[:], sums[c][:])
-                nc.sync.dma_start(out=out_v[:, :, c * P : (c + 1) * P], in_=res[:])
+            if unit == units[-1]:
+                res = ring.tile([P, BLOCKS, HALF], F32, name="res", bufs=2)
+                for k in range(2):
+                    nc.scalar.copy(res[:, spans[k], :], sums[k][:])
+                    nc.sync.dma_start(out=out_v[:, spans[k], :HALF], in_=res[:, spans[k], :])
 
         for i in range(len(units) + 2):
             if i < len(units):
                 weigh(units[i])
             if i >= 2:
                 add_up(units[i - 2])
+
+        product = keep.tile([P, BLOCKS, HALF], F32, name="product")
+        res = ring.tile([P, BLOCKS, HALF], F32, name="res", bufs=2)
+        for b in range(BLOCKS):
+            nc.vector.tensor_tensor(product[:, b, :], picked[TOP - 1][:, b, HALF:], gate_last[:], ALU.mult)
+            if b > 0:
+                span = spans[b - 1]
+                nc.vector.tensor_tensor(res[:, span, :], sums[b + 1][:], product[:, span, :], ALU.add)
+                nc.sync.dma_start(out=out_v[:, span, HALF:], in_=res[:, span, :])

from contextlib import ExitStack

import concourse.mybir as mybir
from concourse.masks import make_identity

K, T, E, C, H, N = 1024, 512, 8, 128, 512, 384
TOP = 4
PAD = 64
P = 128
PASSES = K // 512
BLOCKS = N // P
SLOTS = E * C
HALF = 256
CHUNKS = T // P
FLOPS = 2 * SLOTS * (K * H + H * N)

F32 = mybir.dt.float32
BF16 = mybir.dt.bfloat16
I32 = mybir.dt.int32
U32 = mybir.dt.uint32
U16 = mybir.dt.uint16
U8 = mybir.dt.uint8
FP8X4 = mybir.dt.float8_e4m3fn_x4
FP4X4 = mybir.dt.float4_e2m1fn_x4
ACT = mybir.ActivationFunctionType
ALU = mybir.AluOpType

WORD_GATHERS = [(0, 1), (1, 2), (2, 4), (4, 6), (6, 8)]
BYTE_GATHERS = [(0, 2), (2, 4), (4, 6), (6, 8)]
QUANT_GROUPS = [(0, 4), (4, 6), (6, 7), (7, 8)]
RELU_ON_VECTOR = (7,)
WORD_GROUPS = [(0, 1), (1, 3), (3, 5), (5, 8)]
EARLY = 2


def tile_moe_ecr_mlp_relu2_kernel(
    tc, x_words, x_scales, w1_words, w1_scales, w2_words, w2_scales, gate, offs, pos1, pos2, pos3, pos4, out
):
    nc = tc.nc
    with ExitStack() as ctx:
        keep = ctx.enter_context(tc.tile_pool(name="keep", bufs=1))
        ring = ctx.enter_context(tc.tile_pool(name="ring", bufs=4))
        stream = ctx.enter_context(tc.tile_pool(name="stream", bufs=4))
        psum = ctx.enter_context(tc.psum_pool(name="psum", bufs=1))

        offs_t = keep.tile([P, SLOTS // 16], U16, name="offs_t")
        pos_t = [keep.tile([P, T // 16], U16, name="pos_t%d" % r) for r in range(TOP)]
        xw = keep.tile([P, PASSES * T], I32, name="xw", align_bytes=64)
        xs = keep.tile([P, PASSES * T], U8, name="xs", align_bytes=64)
        early = keep.tile([P, EARLY * PASSES * H], U8, name="early", align_bytes=64)
        late = keep.tile([P, (E - EARLY) * PASSES * H], U8, name="late", align_bytes=64)
        w2s = keep.tile([P, E * N], U8, name="w2s", align_bytes=64)
        y = keep.tile([P, BLOCKS, SLOTS + PAD], F32, name="y", align_bytes=64)
        gate_rows = keep.tile([P, P], F32, name="gate_rows")
        gate_cols = keep.tile([P, TOP * CHUNKS], F32, name="gate_cols")
        ident = keep.tile([P, P], F32, name="ident")

        nc.gpsimd.memset(xs[:].bitcast(I32), 0)
        nc.vector.memset(early[:].bitcast(I32), 0)
        nc.vector.memset(late[:, :2560].bitcast(I32), 0)
        nc.gpsimd.memset(late[:, 2560:].bitcast(I32), 0)
        nc.vector.memset(w2s[:].bitcast(I32), 0)
        make_identity(nc, ident[:])
        nc.vector.memset(gate_rows[:], 0.0)
        nc.vector.memset(y[:, :, SLOTS:], 0.0)

        def load_scales(plane, rows):
            for r in range(4):
                src = rows[r].bitcast(I32)
                dst = plane[r:P:32, :].bitcast(I32).rearrange("q (g w) -> q g w", g=src.shape[1])
                nc.sync.dma_start(out=dst, in_=src)

        def load_words(src):
            groups = src.shape[0] * src.shape[1]
            tile = stream.tile([P, groups * src.shape[3]], U8, name="weights", align_bytes=64)
            nc.sync.dma_start(
                out=tile[:].bitcast(I32).rearrange("p (g w) -> p g w", g=groups),
                in_=src.rearrange("e s p w -> p (e s) w").bitcast(I32),
            )
            return tile

        w1_word = {}
        w1_scale = {}

        def load_w1_words(lo, hi):
            tile = load_words(w1_words[lo:hi])
            for e in range(lo, hi):
                for s in range(PASSES):
                    col = ((e - lo) * PASSES + s) * 2 * H
                    w1_word[e, s] = tile[:, col : col + 2 * H]

        def load_w1_scales(plane, lo, hi):
            load_scales(plane, w1_scales[lo:hi].rearrange("e s (q r) i -> r q (e s) i", r=4))
            for e in range(lo, hi):
                for s in range(PASSES):
                    col = ((e - lo) * PASSES + s) * H
                    w1_scale[e, s] = plane[:, col : col + H]

        nc.sync.dma_start(
            out=xw[:].rearrange("p (s t) -> p s t", s=PASSES),
            in_=x_words.rearrange("s p t r -> p s (t r)").bitcast(I32),
        )
        nc.sync.dma_start(out=offs_t[:], in_=offs)
        nc.sync.dma_start(out=pos_t[0][:], in_=pos1)
        load_scales(xs, x_scales.rearrange("s (q r) t -> r q s t", r=4))
        load_w1_words(0, 1)
        load_w1_scales(early, 0, EARLY)
        load_w1_words(1, 3)
        load_w1_scales(late, EARLY, E)
        load_w1_words(3, 5)
        load_w1_words(5, E)
        load_scales(w2s, w2_scales.rearrange("e o (q r) n -> r q (e o) n", r=4))
        for tile_r, src in zip(pos_t[1:], (pos2, pos3, pos4)):
            nc.sync.dma_start(out=tile_r[:], in_=src)
        nc.sync.dma_start(
            out=gate_rows[: TOP * CHUNKS, :],
            in_=gate.rearrange("r n (c p) -> (r n c) p", p=P)[:: N + 1, :],
        )

        words = {}
        scales = {}

        def gather(found, table, dtype, name, depth, lo, hi):
            idx = offs_t[:, lo * C // 16 : hi * C // 16]
            tile = ring.tile([P, PASSES, (hi - lo) * C], dtype, name=name, align_bytes=64, bufs=depth)
            for s in range(PASSES):
                nc.vector.tensor_copy(tile[:, s, :], table[:, s * T : (s + 1) * T].indirect(idx))
                for e in range(lo, hi):
                    found[e, s] = tile[:, s, (e - lo) * C : (e - lo + 1) * C]

        relu = {}
        hq = {}
        hidden = {}

        def first_layer(e):
            acc = psum.tile([P, H], F32, name="acc", tag="a", bufs=2)
            for s in range(PASSES):
                nc.tensor.matmul_mx(
                    out=acc[:],
                    lhsT=words[e, s].bitcast(FP8X4),
                    lhsT_scale=scales[e, s],
                    rhs=w1_word[e, s].bitcast(FP4X4),
                    rhs_scale=w1_scale[e, s],
                    start=(s == 0),
                    stop=(s == PASSES - 1),
                )
            relu[e] = ring.tile([P, 4, P], F32, name="relu")
            if e in RELU_ON_VECTOR:
                nc.vector.tensor_scalar_max(relu[e][:], acc[:].rearrange("c (m d) -> c d m", d=4), 0.0)
            else:
                nc.scalar.activation(relu[e][:], acc[:].rearrange("c (m d) -> c d m", d=4), ACT.Relu)

        def turn(e):
            turned = psum.tile([P, 4, C], F32, name="turned", tag="b", bufs=2)
            for d in range(4):
                nc.tensor.transpose(turned[:, d, :], relu[e][:, d, :], ident[:])
            lo, hi = [g for g in QUANT_GROUPS if g[0] <= e < g[1]][0]
            if e == lo:
                hidden[lo] = keep.tile([P, hi - lo, C, 4], BF16, name="h%d" % e, align_bytes=64)
            nc.scalar.activation(hidden[lo][:, e - lo, :, :], turned[:].rearrange("p d c -> p c d"), ACT.Square)
            if e == hi - 1:
                codes = keep.tile([P, (hi - lo) * C], U32, name="codes%d" % e, align_bytes=64)
                plane = keep.tile([P, (hi - lo) * C], U8, name="plane%d" % e, align_bytes=64)
                nc.vector.quantize_mx(
                    out=codes[:].bitcast(FP8X4), scales=plane[:], in_=hidden[lo][:].rearrange("p e c d -> p (e c d)")
                )
                for k in range(lo, hi):
                    cols = slice((k - lo) * C, (k - lo + 1) * C)
                    hq[k] = (codes[:, cols], plane[:, cols])

        def second_layer(tag, depth, blocks, pieces):
            lo, hi = pieces[0][1], pieces[-1][2]
            bank = psum.tile([P, len(blocks), (hi - lo) * C], F32, name="acc2", tag=tag, bufs=depth)
            for copy, first, end in pieces:
                for e in range(first, end):
                    codes, plane = hq[e]
                    for b in blocks:
                        col = e * N + b * P
                        nc.tensor.matmul_mx(
                            out=bank[:, b - blocks[0], (e - lo) * C : (e - lo + 1) * C],
                            lhsT=w2w[:, 2 * col : 2 * (col + P)].bitcast(FP4X4),
                            lhsT_scale=w2s[:, col : col + P],
                            rhs=codes.bitcast(FP8X4),
                            rhs_scale=plane,
                            start=True,
                            stop=True,
                        )
                copy(y[:, blocks[0] : blocks[-1] + 1, first * C : end * C], bank[:, :, (first - lo) * C : (end - lo) * C])

        word_starts = dict(WORD_GATHERS)
        byte_starts = dict(BYTE_GATHERS)
        for step in range(E + 1):
            if step in byte_starts:
                gather(scales, xs[:], U8, "gs", 2, step, byte_starts[step])
            if step in word_starts:
                gather(words, xw[:].bitcast(U32), U32, "gw", 2, step, word_starts[step])
            if step < E:
                first_layer(step)
            if step == 0:
                w2w = load_words(w2_words)
            if step == 2:
                gate_last = stream.tile([P, HALF], F32, name="gate_last", tag="weights", align_bytes=64)
                nc.sync.dma_start(out=gate_last[:], in_=gate[TOP - 1, :P, HALF:])
            if 1 <= step <= E:
                turn(step - 1)
        second_layer("c", 4, (0,), [(nc.scalar.copy, 0, 4)])
        second_layer("a", 2, (0,), [(nc.vector.tensor_copy, 4, 7)])
        second_layer("c", 4, (0,), [(nc.vector.tensor_copy, 7, 8)])
        second_layer("b", 2, (1,), [(nc.scalar.copy, 0, 4)])
        second_layer("b", 2, (2,), [(nc.scalar.copy, 0, 4)])
        second_layer("c", 4, (1, 2), [(nc.scalar.copy, 4, 6)])
        second_layer("c", 4, (1, 2), [(nc.scalar.copy, 6, 8)])
        gate_ps = psum.tile([P, P], F32, name="gate_ps", tag="a", bufs=2)
        nc.tensor.transpose(gate_ps[:], gate_rows[:], ident[:])
        nc.scalar.copy(gate_cols[:], gate_ps[:, : TOP * CHUNKS])

        out_v = out.rearrange("(b n) t -> n b t", n=P)
        picked = [ring.tile([P, BLOCKS, T], F32, name="picked", bufs=2) for r in range(TOP)]
        cuts = [(r, 0, T) for r in range(TOP - 1)] + [(TOP - 1, 0, HALF), (TOP - 1, HALF, T)]
        for r, lo, hi in cuts:
            for b in range(BLOCKS):
                nc.vector.tensor_copy(picked[r][:, b, lo:hi], y[:, b, :].indirect(pos_t[r][:, lo // 16 : hi // 16]))

        units = [(r, c) for r in range(TOP) for c in range(CHUNKS)][:-2]
        gated = {}
        sums = [
            psum.tile([P, 2, HALF], F32, name="sums0", tag="b", bufs=2),
            psum.tile([P, 1, HALF], F32, name="sums1", tag="b", bufs=2),
            psum.tile([P, 2, HALF], F32, name="sums2", tag="c", bufs=4),
            psum.tile([P, 1, HALF], F32, name="sums3", tag="c", bufs=4),
        ]
        spans = (slice(0, 2), slice(2, 3))

        first = [psum.tile([P, BLOCKS, P], F32, name="first%d" % c, tag="a", bufs=2) for c in range(2)]
        first.extend([psum.tile([P, BLOCKS, P], F32, name="first%d" % c, tag="c", bufs=4) for c in (2, 3)])
        for b in range(BLOCKS):
            for c in range(CHUNKS):
                nc.tensor.transpose(first[c][:, b, :], picked[0][:, b, c * P : (c + 1) * P], ident[:])

        def weigh(unit):
            r, c = unit
            if r == 0:
                by_token = first[c]
            else:
                if c < 2:
                    by_token = psum.tile([P, BLOCKS, P], F32, name="by_token", tag="a", bufs=2)
                else:
                    by_token = psum.tile([P, BLOCKS, P], F32, name="by_token", tag="c", bufs=4)
                for b in range(BLOCKS):
                    nc.tensor.transpose(by_token[:, b, :], picked[r][:, b, c * P : (c + 1) * P], ident[:])
            gated[unit] = ring.tile([P, BLOCKS, P], F32, name="gated")
            col = r * CHUNKS + c
            nc.scalar.activation(gated[unit][:], by_token[:], ACT.Copy, scale=gate_cols[:, col : col + 1])

        def add_up(unit):
            r, c = unit
            last = TOP - 1 if c < 2 else TOP - 2
            for b in range(BLOCKS):
                nc.tensor.matmul(
                    sums[c // 2 * 2 + b // 2][:, b % 2, c % 2 * P : (c % 2 + 1) * P],
                    lhsT=gated[unit][:, b, :],
                    rhs=ident[:],
                    is_transpose=True,
                    start=(r == 0 and c % 2 == 0 and b != 1),
                    stop=(r == last and c % 2 == 1 and b != 0),
                )
            if unit == units[-1]:
                res = ring.tile([P, BLOCKS, HALF], F32, name="res", bufs=2)
                for k in range(2):
                    nc.scalar.copy(res[:, spans[k], :], sums[k][:])
                    nc.sync.dma_start(out=out_v[:, spans[k], :HALF], in_=res[:, spans[k], :])

        for i in range(len(units) + 2):
            if i < len(units):
                weigh(units[i])
            if i >= 2:
                add_up(units[i - 2])

        product = keep.tile([P, BLOCKS, HALF], F32, name="product")
        res = ring.tile([P, BLOCKS, HALF], F32, name="res", bufs=2)
        for b in range(BLOCKS):
            nc.vector.tensor_tensor(product[:, b, :], picked[TOP - 1][:, b, HALF:], gate_last[:], ALU.mult)
            if b > 0:
                span = spans[b - 1]
                nc.vector.tensor_tensor(res[:, span, :], sums[b + 1][:], product[:, span, :], ALU.add)
                nc.sync.dma_start(out=out_v[:, span, HALF:], in_=res[:, span, :])
